import numpy as np
import ml_dtypes


def mxq(x, axis, fmt="e4m3"):
    dtype, down = {"e4m3": (ml_dtypes.float8_e4m3fn, 7), "e5m2": (ml_dtypes.float8_e5m2, 14)}[fmt]
    v = np.moveaxis(np.asarray(x, np.float32).astype(ml_dtypes.bfloat16).astype(np.float64), axis, -1)
    blocks = v.reshape(v.shape[:-1] + (-1, 32))
    amax = np.abs(blocks).max(-1, keepdims=True)
    byte = np.maximum(np.where(amax > 0, np.frexp(amax)[1] - 1 + 127, 0) - down, 1)
    scale = np.exp2(byte - 127.0)
    codes = (blocks / scale).astype(np.float32).astype(dtype).astype(np.float64)
    return np.moveaxis((codes * scale).reshape(v.shape), -1, axis)


WIDE = False


def mx_kscale(k):
    if not WIDE:
        return np.ones(k)
    levels = np.array([10, -10, 5, -5, 0])
    if k % 512:
        return np.exp2(np.random.permutation(np.resize(levels, k // 32))).repeat(32)
    a = np.empty((k // 512, 16))
    for p in range(k // 512):
        a[p, :8] = np.random.permutation(np.resize(levels, 8))
        for g in range(8):
            far = levels[np.abs(levels - a[p, g]) >= 10]
            a[p, g + 8] = far[np.random.randint(len(far))]
    return np.exp2(a.ravel()).repeat(32)


def f64(x):
    return np.asarray(x).astype(np.float64)


def striped(idx):
    return np.tile(np.asarray(idx).reshape(-1, 16).T, (8, 1)).astype(np.uint16)


def unstriped(offs):
    return offs[:16].T.reshape(-1).astype(np.int64)


E2M1 = np.array([0.0, 0.5, 1.0, 1.5, 2.0, 3.0, 4.0, 6.0, -0.0, -0.5, -1.0, -1.5, -2.0, -3.0, -4.0, -6.0])


def pack_weight(w, fmt):
    k, n = w.shape
    w = f64(np.asarray(w, np.float32).astype(ml_dtypes.bfloat16)).reshape(k // 32, 32, n)
    amax = np.abs(w).max(1)
    if fmt == "e4m3":
        byte = np.frexp(amax)[1] - 1 + 127 - 7
    else:
        mant, ex = np.frexp(amax / 6.0)
        byte = np.where(mant > 0.5, ex, ex - 1) + 127
    byte = np.clip(np.where(amax > 0, byte, 1), 1, 254)
    scaled = (w * np.exp2(127.0 - byte)[:, None, :]).reshape(k, n).astype(np.float32)
    by_word = np.ascontiguousarray(scaled.reshape(k // 512, 128, 4, n).transpose(0, 1, 3, 2))
    if fmt == "e4m3":
        words = by_word.astype(ml_dtypes.float8_e4m3fn).view(np.uint8)
    else:
        c = by_word.astype(ml_dtypes.float4_e2m1fn).view(np.uint8) & 0xF
        words = (c[..., 0::2] | (c[..., 1::2] << 4)).reshape(k // 512, 128, 2 * n)
    return np.ascontiguousarray(words), np.ascontiguousarray(byte.astype(np.uint8).reshape(k // 512, 16, n))


def unpack_weight(words, scales, fmt):
    g, _, n = scales.shape
    words = np.ascontiguousarray(words).reshape(g, 128, n, -1)
    if fmt == "e4m3":
        vals = words.view(ml_dtypes.float8_e4m3fn).astype(np.float64)
    else:
        nib = np.empty((g, 128, n, 4), np.uint8)
        nib[..., 0::2] = words & 0xF
        nib[..., 1::2] = words >> 4
        vals = E2M1[nib]
    vals = vals * np.repeat(np.exp2(scales.astype(np.float64) - 127.0), 8, axis=1)[..., None]
    return vals.transpose(0, 1, 3, 2).reshape(g * 512, n)


def softplus(v):
    return np.log(1.0 + np.exp(v))


def sigmoid(v):
    return 1.0 / (1.0 + np.exp(-v))


K, R, F, T, J, M = 512, 128, 512, 2048, 512, 256


def setup_inputs():
    n = np.random.standard_normal
    idx = np.random.permutation(T)[:J]
    idx2 = np.random.permutation(J)[:M]
    idx3 = np.random.permutation(J)[:M]
    fk = mx_kscale(K)
    ff = mx_kscale(F)
    tabp = pack_weight(n((K, T)) / fk[:, None], "e2m1")
    dtabp = pack_weight(n((K, T)) / fk[:, None], "e2m1")
    return {
        "tab_words": tabp[0],
        "tab_scales": tabp[1],
        "w1": (n((K, R)) * 1 / np.sqrt(K) * fk[:, None]).astype(np.float32),
        "floor": (np.random.uniform(0.2, 0.8, (R, 1))).astype(np.float32),
        "wo": (n((F, R)) * 1 / np.sqrt(F) * ff[:, None]).astype(np.float32),
        "dy": (n((F, M)) / ff[:, None]).astype(np.float32),
        "dtab_words": dtabp[0],
        "dtab_scales": dtabp[1],
        "og": (np.random.uniform(0.7, 2.0, (R, 1))).astype(np.float32),
        "base": (0.3 * n((R, J))).astype(np.float32),
        "offs": striped(idx),
        "offs2": striped(idx2),
        "offs3": striped(idx3),
    }


def reference(tab_words, tab_scales, w1, floor, wo, dy, dtab_words, dtab_scales, og, base, offs, offs2, offs3):
    idx = unstriped(offs)
    idx2 = unstriped(offs2)
    idx3 = unstriped(offs3)
    tabu = unpack_weight(tab_words, tab_scales, "e2m1")
    dtabu = unpack_weight(dtab_words, dtab_scales, "e2m1")
    w1q = mxq(f64(w1), 0, "e4m3")
    tabidxg = tabu[:, idx]
    a = w1q.T @ tabidxg
    dtabidxg = dtabu[:, idx]
    ta = w1q.T @ dtabidxg
    h0 = softplus(a)
    h1 = np.log(h0 + f64(floor))
    woq = mxq(f64(wo), 0, "e4m3")
    dyq = mxq(f64(dy), 0, "e4m3")
    c0 = woq.T @ dyq
    e1 = c0 * sigmoid(h1[:, idx2])
    s1 = np.zeros((R, J))
    s1[:, idx2] = e1
    e2 = c0 * (h1[:, idx2] - h1[:, idx3]) * sigmoid(h1[:, idx2]) * (1.0 - sigmoid(h1[:, idx2]))
    s2 = np.zeros((R, J))
    s2[:, idx2] = e2
    e3 = c0 * sigmoid(h1[:, idx2]) * (-1.0)
    s3 = np.zeros((R, J))
    s3[:, idx3] = e3
    dh1 = s1 + s2 + s3
    dh0 = dh1 / (h0 + f64(floor))
    xh0 = ta * sigmoid(a)
    xh1 = xh0 / (h0 + f64(floor))
    xe1 = xh1[:, idx2] * sigmoid(h1[:, idx2]) * (1.0 - sigmoid(h1[:, idx2])) * c0
    xs1 = np.zeros((R, J))
    xs1[:, idx2] = xe1
    xe2 = ((xh1[:, idx2] - xh1[:, idx3]) * c0 * sigmoid(h1[:, idx2]) + xh1[:, idx2] * sigmoid(h1[:, idx2]) * (1.0 - sigmoid(h1[:, idx2])) * c0 * (h1[:, idx2] - h1[:, idx3])) * (1.0 - sigmoid(h1[:, idx2])) + xh1[:, idx2] * sigmoid(h1[:, idx2]) * (1.0 - sigmoid(h1[:, idx2])) * (-1.0) * c0 * (h1[:, idx2] - h1[:, idx3]) * sigmoid(h1[:, idx2])
    xs2 = np.zeros((R, J))
    xs2[:, idx2] = xe2
    xe3 = xh1[:, idx2] * sigmoid(h1[:, idx2]) * (1.0 - sigmoid(h1[:, idx2])) * c0 * (-1.0)
    xs3 = np.zeros((R, J))
    xs3[:, idx3] = xe3
    xdh1 = xs1 + xs2 + xs3
    xdh0 = (xdh1 - xh0 * dh1 / (h0 + f64(floor))) / (h0 + f64(floor))
    xda = xdh0 * sigmoid(a) + ta * sigmoid(a) * (1.0 - sigmoid(a)) * dh0
    y = xda * f64(og) + f64(base)
    return y

from contextlib import ExitStack

import concourse.mybir as mybir

K, R, F, T, J, M = 512, 128, 512, 2048, 512, 256
FLOPS = 2 * K * R * J * 2 + 2 * F * R * M

F32 = mybir.dt.float32
BF16 = mybir.dt.bfloat16
I32 = mybir.dt.int32
U32 = mybir.dt.uint32
U16 = mybir.dt.uint16
U8 = mybir.dt.uint8
FP8X4 = mybir.dt.float8_e4m3fn_x4
FP4X4 = mybir.dt.float4_e2m1fn_x4
ACT = mybir.ActivationFunctionType
ALU = mybir.AluOpType

P = 128
PACK = 4
HALF = J // 2
QUARTER = J // 4


def tile_attend_hvclogratios_kernel(tc, tab_words, tab_scales, w1, floor, wo, dy, dtab_words, dtab_scales,
                                     og, base, offs, offs2, offs3, out):
    nc = tc.nc
    vec, act = nc.vector, nc.scalar
    with ExitStack() as ctx:
        sb = ctx.enter_context(tc.tile_pool(name="sb", bufs=1))
        ps = ctx.enter_context(tc.psum_pool(name="ps", bufs=1))

        def f32(name, width, tag=""):
            return sb.tile([P, width], F32, name=name, tag=tag or name, align_bytes=64)

        def load_scale_rows(queue, plane, scales):
            for q in range(4):
                queue.dma_start(out=plane[32 * q : 32 * q + 4, :].bitcast(I32),
                                in_=scales[0, 4 * q : 4 * q + 4, :].bitcast(I32))

        def load_rows(queue, name, src, width):
            raw = sb.tile([P, PACK, width], F32, name=name, align_bytes=64)
            queue.dma_start(out=raw[:], in_=src.rearrange("(p t) c -> p t c", t=PACK))
            return raw

        def interleave(copy, name, raw, width):
            grouped = sb.tile([P, width, PACK], BF16, name=name, align_bytes=64)
            copy(out=grouped[:].rearrange("p (c i) t -> p c t i", i=4),
                 in_=raw[:].rearrange("p t (c i) -> p c t i", i=4))
            return grouped

        def interleave_on_gpsimd(name, raw, width):
            grouped = sb.tile([P, width, PACK], BF16, name=name, align_bytes=64)
            nc.gpsimd.tensor_scalar(out=grouped[:], in0=raw[:].rearrange("p t c -> p c t"), scalar1=1.0, scalar2=0.0,
                                    op0=ALU.mult, op1=ALU.add)
            return grouped

        def quantize(name, grouped, width, tag=""):
            codes = sb.tile([P, width], U32, name=name + "_codes", tag=tag or name, align_bytes=64)
            scales = sb.tile([P, width], U8, name=name + "_scales", align_bytes=64)
            vec.quantize_mx(out=codes[:].bitcast(FP8X4), scales=scales[:],
                            in_=grouped[:].rearrange("p c t -> p (c t)"))
            return codes, scales

        list1 = sb.tile([P, J // 16], U16, name="list1")
        list2 = sb.tile([P, M // 16], U16, name="list2")
        list3 = sb.tile([P, M // 16], U16, name="list3")
        tab_w = sb.tile([P, T], U16, name="tab_w", align_bytes=64)
        tab_s = sb.tile([P, T], U8, name="tab_s", tag="tab_s", align_bytes=64)
        dtab_w = sb.tile([P, T], U16, name="dtab_w", align_bytes=64)
        dtab_s = sb.tile([P, T], U8, name="dtab_s", align_bytes=64)
        floor_c = f32("floor_c", 1)
        og_c = f32("og_c", 1)
        base_t = f32("base_t", J)

        vec.memset(tab_s[:, : T // 2].bitcast(I32), 0)
        nc.gpsimd.memset(tab_s[:, T // 2 :].bitcast(I32), 0)
        nc.gpsimd.memset(dtab_s[:].bitcast(I32), 0)
        nc.sync.dma_start(list1[:], offs)
        nc.sync.dma_start(out=tab_w[:].bitcast(I32), in_=tab_words[0].bitcast(I32))
        w1_raw = load_rows(nc.sync, "w1_raw", w1, R)
        load_scale_rows(nc.sync, tab_s, tab_scales)
        nc.sync.dma_start(list2[:], offs2)
        nc.sync.dma_start(list3[:], offs3)
        nc.sync.dma_start(out=dtab_w[:].bitcast(I32), in_=dtab_words[0].bitcast(I32))
        load_scale_rows(nc.sync, dtab_s, dtab_scales)
        dy_raw = load_rows(nc.sync, "dy_raw", dy, M)
        wo_raw = load_rows(nc.sync, "wo_raw", wo, R)
        nc.gpsimd.dma_start(out=floor_c[:], in_=floor)
        nc.gpsimd.dma_start(out=og_c[:], in_=og)
        nc.sync.dma_start(out=base_t[:], in_=base)

        e2_at = f32("e2_at", J)
        e3_at = f32("e3_at", J)
        x2_at = f32("x2_at", J)
        x3_at = f32("x3_at", J)
        for window in (e2_at, e3_at, x2_at, x3_at):
            vec.memset(window[:], 0.0)

        halves = [slice(h * HALF, (h + 1) * HALF) for h in range(2)]
        list1_halves = [list1[:, h * (HALF // 16) : (h + 1) * (HALF // 16)] for h in range(2)]

        def across(ap, c):
            return ap.rearrange("p (h c x) -> p h c x", h=2, c=2)[:, :, c, :]

        tab_gs = sb.tile([P, J], U8, name="tab_gs", align_bytes=64)
        tab_gw = sb.tile([P, J], U16, name="tab_gw", align_bytes=64)
        for h in range(2):
            vec.tensor_copy(out=tab_gw[:, halves[h]], in_=tab_w[:].indirect(list1_halves[h]))
        vec.tensor_copy(out=tab_gs[:, halves[0]], in_=tab_s[:].indirect(list1_halves[0]))
        w1_codes, w1_scales = quantize("w1", interleave(act.copy, "w1_bf", w1_raw, R), R)
        vec.tensor_copy(out=tab_gs[:, halves[1]], in_=tab_s[:].indirect(list1_halves[1]))
        a_ps = [ps.tile([P, HALF], F32, name="a_ps%d" % h) for h in range(2)]
        th = f32("th", J)
        th_abs = f32("th_abs", J)
        for h in range(2):
            nc.tensor.matmul_mx(out=a_ps[h][:], lhsT=w1_codes[:].bitcast(FP8X4), lhsT_scale=w1_scales[:],
                                rhs=tab_gw[:, halves[h]].bitcast(FP4X4), rhs_scale=tab_gs[:, halves[h]],
                                start=True, stop=True)
            act.activation(out=th[:, halves[h]], in_=a_ps[h][:], func=ACT.Tanh, scale=0.5)
            act.activation(out=th_abs[:, halves[h]], in_=th[:, halves[h]], func=ACT.Abs)

        dtab_gs = sb.tile([P, J], U8, name="dtab_gs", align_bytes=64)
        dtab_gw = sb.tile([P, J], U16, name="dtab_gw", align_bytes=64)
        vec.tensor_copy(out=dtab_gw[:], in_=dtab_w[:].indirect(list1[:]))
        ta_ps = [ps.tile([P, HALF], F32, name="ta_ps%d" % h) for h in range(2)]
        for h in range(2):
            vec.tensor_copy(out=dtab_gs[:, halves[h]], in_=dtab_s[:].indirect(list1_halves[h]))
            nc.tensor.matmul_mx(out=ta_ps[h][:], lhsT=w1_codes[:].bitcast(FP8X4), lhsT_scale=w1_scales[:],
                                rhs=dtab_gw[:, halves[h]].bitcast(FP4X4), rhs_scale=dtab_gs[:, halves[h]],
                                start=True, stop=True)
        tn = f32("tn", J)
        for h in range(2):
            vec.scalar_tensor_tensor(out=tn[:, halves[h]], in0=th[:, halves[h]], scalar=1.0, in1=ta_ps[h][:],
                                     op0=ALU.subtract, op1=ALU.mult)

        ln_sig = f32("ln_sig", J)
        h0 = f32("h0", J, tag="th")
        h1 = f32("h1", J)
        for c in range(2):
            act.activation(out=across(ln_sig[:], c), in_=across(th_abs[:], c), func=ACT.Ln, scale=0.5, bias=0.5)
        for c in range(2):
            for h in range(2):
                cols = slice(h * HALF + c * QUARTER, h * HALF + (c + 1) * QUARTER)
                vec.scalar_tensor_tensor(out=h0[:, cols], in0=a_ps[h][:, c * QUARTER : (c + 1) * QUARTER], scalar=0.0,
                                         in1=ln_sig[:, cols], op0=ALU.max, op1=ALU.subtract)
            act.activation(out=across(h1[:], c), in_=across(h0[:], c), func=ACT.Ln, bias=floor_c[:])

        dy_bf = interleave_on_gpsimd("dy_bf", dy_raw, M)
        wo_bf = interleave_on_gpsimd("wo_bf", wo_raw, R)

        ln_sa = f32("ln_sa", J)
        ln_q = f32("ln_q", J)
        for h in range(2):
            vec.tensor_tensor(out=ln_sa[:, halves[h]], in0=a_ps[h][:], in1=h0[:, halves[h]], op=ALU.subtract)
        g2 = f32("g2", M)
        nd = f32("nd", M)
        vec.tensor_copy(out=g2[:], in_=h1[:].indirect(list2[:]))
        dy_codes, dy_scales = quantize("dy", dy_bf, M)
        wo_codes, wo_scales = quantize("wo", wo_bf, R)
        for c in halves:
            vec.tensor_tensor(out=ln_q[:, c], in0=ln_sa[:, c], in1=h1[:, c], op=ALU.subtract)
        c0_ps = ps.tile([P, M], F32, name="c0_ps")
        nc.tensor.matmul_mx(out=c0_ps[:], lhsT=wo_codes[:].bitcast(FP8X4), lhsT_scale=wo_scales[:],
                            rhs=dy_codes[:].bitcast(FP8X4), rhs_scale=dy_scales[:], start=True, stop=True)
        vec.tensor_tensor(out=nd[:], in0=h1[:].indirect(list3[:]), in1=g2[:], op=ALU.subtract)

        q = f32("q", J)
        th2 = f32("th2", M)
        act.activation(out=th2[:], in_=g2[:], func=ACT.Tanh, scale=0.5)
        act.activation(out=q[:, halves[0]], in_=ln_q[:, halves[0]], func=ACT.Exp)
        act.activation(out=q[:, halves[1]], in_=ln_q[:, halves[1]], func=ACT.Exp)

        xh1 = f32("xh1", J)
        alpha = f32("alpha", M)
        kk = f32("kk", M)
        mm = f32("mm", M)
        e12 = f32("e12", M)
        vv = f32("vv", M)

        def make_xh1(h):
            vec.tensor_tensor(out=xh1[:, halves[h]], in0=ta_ps[h][:], in1=q[:, halves[h]], op=ALU.mult)

        vec.scalar_tensor_tensor(out=alpha[:], in0=th2[:], scalar=1.0, in1=c0_ps[:], op0=ALU.add, op1=ALU.mult)
        act.activation(out=e3_at[:].indirect(list3[:]), in_=alpha[:], func=ACT.Copy, scale=-0.5)
        vec.scalar_tensor_tensor(out=kk[:], in0=th2[:], scalar=1.0, in1=nd[:], op0=ALU.subtract, op1=ALU.mult)
        make_xh1(0)
        make_xh1(1)
        vec.scalar_tensor_tensor(out=e12[:], in0=kk[:], scalar=2.0, in1=alpha[:], op0=ALU.add, op1=ALU.mult)
        act.activation(out=e2_at[:].indirect(list2[:]), in_=e12[:], func=ACT.Copy, scale=0.25)
        vec.scalar_tensor_tensor(out=mm[:], in0=th2[:], scalar=1.0, in1=alpha[:], op0=ALU.subtract, op1=ALU.mult)
        vec.scalar_tensor_tensor(out=vv[:], in0=kk[:], scalar=2.0, in1=nd[:], op0=ALU.add, op1=ALU.add)
        xe3 = f32("xe3", M)
        z3 = f32("z3", M)
        yy = f32("yy", M)
        xe12 = f32("xe12", M)
        vec.tensor_tensor(out=xe3[:], in0=xh1[:].indirect(list2[:]), in1=mm[:], op=ALU.mult)
        act.activation(out=x3_at[:].indirect(list3[:]), in_=xe3[:], func=ACT.Copy, scale=0.25)
        vec.tensor_tensor(out=z3[:], in0=xh1[:].indirect(list3[:]), in1=mm[:], op=ALU.mult)
        vec.tensor_tensor(out=yy[:], in0=xe3[:], in1=vv[:], op=ALU.mult)
        cn = f32("cn", J)
        vec.scalar_tensor_tensor(out=cn[:, halves[0]], in0=xh1[:, halves[0]], scalar=2.0, in1=tn[:, halves[0]], op0=ALU.mult, op1=ALU.add)
        vec.tensor_tensor(out=xe12[:], in0=z3[:], in1=yy[:], op=ALU.subtract)
        act.activation(out=x2_at[:].indirect(list2[:]), in_=xe12[:], func=ACT.Copy, scale=0.25)
        vec.scalar_tensor_tensor(out=cn[:, halves[1]], in0=xh1[:, halves[1]], scalar=2.0, in1=tn[:, halves[1]], op0=ALU.mult, op1=ALU.add)

        dh1 = f32("dh1", J, tag="yy")
        s1 = f32("s1", J)
        s2 = f32("s2", J)
        s3 = f32("s3", J)
        s4 = f32("s4", J)
        res = f32("res", J)
        vec.tensor_tensor(out=dh1[:], in0=e2_at[:], in1=e3_at[:], op=ALU.add)
        for c in halves:
            vec.scalar_tensor_tensor(out=s1[:, c], in0=dh1[:, c], scalar=-0.5, in1=cn[:, c], op0=ALU.mult, op1=ALU.mult)
        for c in halves:
            vec.tensor_tensor(out=s2[:, c], in0=s1[:, c], in1=x3_at[:, c], op=ALU.add)
        for c in halves:
            vec.tensor_tensor(out=s3[:, c], in0=s2[:, c], in1=x2_at[:, c], op=ALU.add)
        for c in halves:
            vec.scalar_tensor_tensor(out=s4[:, c], in0=s3[:, c], scalar=og_c[:], in1=q[:, c], op0=ALU.mult, op1=ALU.mult)
        for c in halves:
            vec.tensor_tensor(out=res[:, c], in0=s4[:, c], in1=base_t[:, c], op=ALU.add)
            nc.sync.dma_start(out=out[:, c], in_=res[:, c])
